import numpy as np
import ml_dtypes


def mxq(x, axis, fmt="e4m3"):
    dtype, down = {"e4m3": (ml_dtypes.float8_e4m3fn, 7), "e5m2": (ml_dtypes.float8_e5m2, 14)}[fmt]
    v = np.moveaxis(np.asarray(x, np.float32).astype(ml_dtypes.bfloat16).astype(np.float64), axis, -1)
    blocks = v.reshape(v.shape[:-1] + (-1, 32))
    amax = np.abs(blocks).max(-1, keepdims=True)
    byte = np.maximum(np.where(amax > 0, np.frexp(amax)[1] - 1 + 127, 0) - down, 1)
    scale = np.exp2(byte - 127.0)
    codes = (blocks / scale).astype(np.float32).astype(dtype).astype(np.float64)
    return np.moveaxis((codes * scale).reshape(v.shape), -1, axis)


WIDE = False


def mx_kscale(k, group=512):
    if not WIDE:
        return np.ones(k)
    levels = np.array([10, -10, 5, -5, 0])
    if group != 512:
        return np.exp2(np.random.permutation(np.resize(levels, k // group))).repeat(group)
    if k % 512:
        return np.exp2(np.random.permutation(np.resize(levels, k // 32))).repeat(32)
    a = np.empty((k // 512, 16))
    for p in range(k // 512):
        a[p, :8] = np.random.permutation(np.resize(levels, 8))
        for g in range(8):
            far = levels[np.abs(levels - a[p, g]) >= 10]
            a[p, g + 8] = far[np.random.randint(len(far))]
    return np.exp2(a.ravel()).repeat(32)


def f64(x):
    return np.asarray(x).astype(np.float64)


def striped(idx):
    return np.tile(np.asarray(idx).reshape(-1, 16).T, (8, 1)).astype(np.uint16)


def unstriped(offs):
    return offs[:16].T.reshape(-1).astype(np.int64)


H, KV, D, NQ, N = 4, 1, 128, 512, 512


def setup_inputs():
    n = np.random.standard_normal
    s = mx_kscale(D, 0)[:, None]
    u = mx_kscale(N)
    t = np.random.uniform(0.5, 2.0, N) * u
    v = n((KV, N, 128))
    return {
        "qT": (n((H, D, NQ)) * s * (0.70 / np.sqrt(D))).astype(np.float32),
        "kT": (n((KV, D, N)) / s).astype(np.float32),
        "t": t.reshape(N, 1).astype(np.float32),
        "v": (v / t[:, None]).astype(np.float32),
        "og": n((H, NQ, 128)).astype(np.float32),
    }


def reference(qT, kT, t, v, og):
    a = np.repeat(mxq(f64(kT), 1, "e4m3"), H // KV, 0).transpose(0, 2, 1) @ mxq(f64(qT), 1, "e4m3")
    p = a / (1.0 + np.exp(-a))
    w = p * f64(t)
    y = mxq(w, 1, "e4m3").transpose(0, 2, 1) @ np.repeat(mxq(f64(v), 1, "e4m3"), H // KV, 0)
    y = y / 16.0
    y = y / (1.0 + np.exp(-f64(og)))
    return y

@@ -1,0 +1,213 @@
+from contextlib import ExitStack
+
+import concourse.mybir as mybir
+
+H, D, NQ, N, E = 4, 128, 512, 512, 128
+FLOPS = 2 * H * NQ * N * (D + E)
+
+F32 = mybir.dt.float32
+BF16 = mybir.dt.bfloat16
+U32 = mybir.dt.uint32
+I32 = mybir.dt.int32
+U8 = mybir.dt.uint8
+FP8X4 = mybir.dt.float8_e4m3fn_x4
+ACT = mybir.ActivationFunctionType
+ALU = mybir.AluOpType
+
+P = 128
+PACK = 4
+ROWS = 32
+QT = 128
+CHUNKS = NQ // QT
+K_VECTOR = 88
+LEAD = 3
+
+
+def tile_rows_a_silu_gate_kernel(tc, qT, kT, t, v, og, out):
+    nc = tc.nc
+    steps = [(0, c) for c in range(CHUNKS)] + [(h, c) for c in range(CHUNKS) for h in range(1, H)]
+    groups = [[0, 1, 2, 3], [4, 5, 6], [7, 8, 9], [10, 11, 12], [13, 14], [15]]
+
+    with ExitStack() as ctx:
+        sb = ctx.enter_context(tc.tile_pool(name="sb", bufs=1))
+        ps = ctx.enter_context(tc.psum_pool(name="ps", bufs=1))
+        ctx.enter_context(tc.manual_schedule())
+
+        q_rows = qT.rearrange("h (p j) n -> (h p) j n", j=PACK)
+        q_raw0 = sb.tile([P, PACK, QT], F32, name="q_raw0")
+        q_raw1 = sb.tile([P, PACK, QT], F32, name="q_raw1")
+        q_raw23 = sb.tile([P, PACK, 2 * QT], F32, name="q_raw23")
+        q_raw = [q_raw0[:], q_raw1[:], q_raw23[:, :, 0:QT], q_raw23[:, :, QT : 2 * QT]]
+        k_raw = sb.tile([ROWS, PACK, N], F32, name="k_raw")
+        t_sb = sb.tile([P, PACK], F32, name="t_sb")
+        v_raw = sb.tile([P, PACK, E], F32, name="v_raw")
+        og_first = sb.tile([P, CHUNKS, E], F32, name="og_first")
+        og_rest = sb.tile([P, H - 1, CHUNKS, E], F32, name="og_rest")
+
+        nc.sync.dma_start(out=q_raw0[:], in_=q_rows[:, :, 0:QT])
+        nc.sync.dma_start(out=k_raw[:], in_=kT[0].rearrange("(p j) n -> p j n", j=PACK))
+        nc.sync.dma_start(out=t_sb[:], in_=t.rearrange("(s r) o -> s (r o)", r=PACK))
+        nc.sync.dma_start(out=q_raw1[:], in_=q_rows[:, :, QT : 2 * QT])
+        nc.sync.dma_start(out=q_raw23[:], in_=q_rows[:, :, 2 * QT : 4 * QT])
+        nc.sync.dma_start(out=v_raw[:], in_=v[0].rearrange("(s r) e -> s r e", r=PACK))
+
+        k_pack = sb.tile([P, N + N // PACK], U32, name="k_pack", align_bytes=64)
+        k_codes = k_pack[:, 0:N].bitcast(FP8X4)
+        k_scales = k_pack[:, N : N + N // PACK].bitcast(U8)
+        nc.vector.memset(k_pack[0:ROWS, N : N + N // PACK].bitcast(I32), 0)
+
+        warm = sb.tile([P, 2], F32, name="warm")
+        nc.vector.memset(warm[:, 0:1], 0.0)
+        nc.scalar.activation(out=warm[:, 1:2], in_=warm[:, 0:1], func=ACT.Silu)
+
+        q_bf = [sb.tile([P, QT, PACK], BF16, name="q_bf%d" % c, align_bytes=64) for c in range(CHUNKS)]
+        q_codes = [sb.tile([P, QT], U32, name="q_codes%d" % c, align_bytes=64) for c in range(CHUNKS)]
+        q_scales = [sb.tile([P, QT], U8, name="q_scales%d" % c, align_bytes=64) for c in range(CHUNKS)]
+        k_bf = sb.tile([ROWS, PACK, P, PACK], BF16, name="k_bf", align_bytes=64)
+        v_bf = sb.tile([P, E, PACK], BF16, name="v_bf", align_bytes=64)
+        v_codes = sb.tile([P, E], U32, name="v_codes", align_bytes=64)
+        v_scales = sb.tile([P, E], U8, name="v_scales", align_bytes=64)
+        p_sb = [sb.tile([P, QT, PACK], F32, name="p%d" % i) for i in range(len(steps))]
+        w_bf = [sb.tile([P, QT, PACK], BF16, name="w_bf%d" % i, align_bytes=64) for i in range(len(steps))]
+        w_codes = [sb.tile([P, QT], U32, name="w_codes%d" % i, align_bytes=64) for i in range(len(steps))]
+        w_scales = [sb.tile([P, QT], U8, name="w_scales%d" % i, align_bytes=64) for i in range(len(steps))]
+        gate_first = sb.tile([P, CHUNKS, E], F32, name="gate_first")
+        gate_rest = [sb.tile([P, H - 1, E], F32, name="gate_rest%d" % c) for c in range(CHUNKS)]
+        res = [sb.tile([P, len(g), E], F32, name="res%d" % n) for n, g in enumerate(groups)]
+
+        score_banks = [ps.tile([P, PACK * QT], F32, name="score%d" % b) for b in range(H + 1)]
+        y_banks = [ps.tile([P, PACK * E], F32, name="y%d" % b) for b in range(3)]
+
+        def words_out(tile):
+            return tile[:].rearrange("p (c i) j -> p c j i", i=4)
+
+        def words_in(raw):
+            return raw.rearrange("p j (c i) -> p c j i", i=4)
+
+        def quantize(codes, scales, values):
+            nc.vector.quantize_mx(out=codes, scales=scales, in_=values)
+
+        def quantize_q(c):
+            quantize(q_codes[c][:].bitcast(FP8X4), q_scales[c][:], q_bf[c][:].rearrange("p n j -> p (n j)"))
+
+        def bank_of(i):
+            h, c = steps[i]
+            return score_banks[c % 2] if h == 0 else score_banks[h + 1]
+
+        def scores(i):
+            h, c = steps[i]
+            rows = slice(ROWS * h, ROWS * (h + 1))
+            for r in range(PACK):
+                cols = slice(P * r, P * (r + 1))
+                nc.tensor.matmul_mx(
+                    out=bank_of(i)[:, QT * r : QT * (r + 1)],
+                    lhsT=k_codes[rows, cols],
+                    lhsT_scale=k_scales[rows, cols],
+                    rhs=q_codes[c][rows, :].bitcast(FP8X4),
+                    rhs_scale=q_scales[c][rows, :],
+                    start=True,
+                    stop=True,
+                )
+
+        def silu(i):
+            nc.scalar.activation(out=p_sb[i][:], in_=bank_of(i)[:].rearrange("p (r n) -> p n r", r=PACK), func=ACT.Silu)
+
+        def weigh(i):
+            nc.vector.tensor_tensor(
+                out=w_bf[i][:],
+                in0=p_sb[i][:],
+                in1=t_sb[:, 0:PACK].unsqueeze(1).to_broadcast([P, QT, PACK]),
+                op=ALU.mult,
+            )
+
+        def group_of(i):
+            return [n for n, g in enumerate(groups) if i in g][0]
+
+        def values(i):
+            quantize(w_codes[i][:].bitcast(FP8X4), w_scales[i][:], w_bf[i][:].rearrange("p n j -> p (n j)"))
+            n = group_of(i)
+            slot = groups[n].index(i)
+            nc.tensor.matmul_mx(
+                out=y_banks[n % 3][:, E * slot : E * (slot + 1)],
+                lhsT=w_codes[i][:].bitcast(FP8X4),
+                lhsT_scale=w_scales[i][:],
+                rhs=v_codes[:].bitcast(FP8X4),
+                rhs_scale=v_scales[:],
+                start=True,
+                stop=True,
+            )
+
+        def finish(n, queue):
+            g = groups[n]
+            h0, c0 = steps[g[0]]
+            if h0 == 0:
+                gate = gate_first[:]
+                dst = out[0].rearrange("(c m) e -> m c e", m=QT)
+            else:
+                gate = gate_rest[c0][:, h0 - 1 : h0 - 1 + len(g), :]
+                dst = out[h0 : h0 + len(g), QT * c0 : QT * (c0 + 1), :].rearrange("h m e -> m h e")
+            nc.vector.scalar_tensor_tensor(
+                out=res[n][:].rearrange("p g e -> p (g e)"),
+                in0=gate.rearrange("p g e -> p (g e)"),
+                scalar=1.0,
+                in1=y_banks[n % 3][:, 0 : E * len(g)],
+                op0=ALU.add,
+                op1=ALU.mult,
+            )
+            queue.dma_start(out=dst, in_=res[n][:])
+
+        nc.vector.tensor_copy(out=words_out(q_bf[0]), in_=words_in(q_raw[0]))
+        k_src = k_raw[:].rearrange("p j (s r) -> p s r j", r=PACK)
+        k_dst = k_bf[:].rearrange("p r s j -> p s r j")
+        quantize_q(0)
+        nc.vector.tensor_copy(out=k_dst[:, 0:K_VECTOR, :, :], in_=k_src[:, 0:K_VECTOR, :, :])
+        nc.scalar.copy(out=k_dst[:, K_VECTOR:P, :, :], in_=k_src[:, K_VECTOR:P, :, :])
+        nc.scalar.copy(out=words_out(q_bf[1]), in_=words_in(q_raw[1]))
+        for r in range(PACK):
+            cols = slice(P * r, P * (r + 1))
+            quantize(k_codes[0:ROWS, cols], k_scales[0:ROWS, cols], k_bf[:, r, :, :].rearrange("p s j -> p (s j)"))
+        for h in range(1, H):
+            nc.sync.dma_start(out=k_pack[ROWS * h : ROWS * (h + 1), :].bitcast(I32), in_=k_pack[0:ROWS, :].bitcast(I32))
+        nc.sync.dma_start(out=og_first[:], in_=og[0].rearrange("(c m) e -> m c e", m=QT))
+        nc.sync.dma_start(
+            out=og_rest[:].rearrange("m h c e -> m (h c) e"),
+            in_=og[1:H].rearrange("h (c m) e -> m (h c) e", m=QT),
+        )
+        quantize_q(1)
+        nc.vector.tensor_copy(out=words_out(q_bf[2]), in_=words_in(q_raw[2]))
+        scores(0)
+        silu(0)
+        scores(1)
+        silu(1)
+        nc.scalar.copy(out=words_out(q_bf[3]), in_=words_in(q_raw[3]))
+        quantize_q(2)
+        scores(2)
+        silu(2)
+        nc.scalar.activation(out=words_out(v_bf), in_=words_in(v_raw[:]), func=ACT.Copy, scale=1.0 / 32.0)
+
+        gates_after = {5: -1, 7: 0, 9: 1, 11: 2, 13: 3}
+        finish_after = {5: 0, 8: 1, 11: 2, 14: 3}
+        for i in range(len(steps)):
+            if i == 0:
+                weigh(0)
+                quantize_q(3)
+            j = i + LEAD
+            if j < len(steps):
+                scores(j)
+                silu(j)
+                if j in gates_after:
+                    c = gates_after[j]
+                    if c < 0:
+                        nc.scalar.activation(out=gate_first[:], in_=og_first[:], func=ACT.Tanh, scale=0.5)
+                    else:
+                        nc.scalar.activation(out=gate_rest[c][:], in_=og_rest[:, :, c, :], func=ACT.Tanh, scale=0.5)
+            if i > 0:
+                weigh(i)
+                if i == 1:
+                    quantize(v_codes[:].bitcast(FP8X4), v_scales[:], v_bf[:].rearrange("p e j -> p (e j)"))
+                values(i - 1)
+            if i in finish_after:
+                finish(finish_after[i], nc.sync)
+        values(len(steps) - 1)
+        finish(4, nc.sync)
+        finish(5, nc.scalar)

@@ -49,7 +49,6 @@ def tile_rows_a_silu_gate_kernel(tc, qT, kT, t, v, og, out):
         nc.sync.dma_start(out=t_sb[:], in_=t.rearrange("(s r) o -> s (r o)", r=PACK))
         nc.sync.dma_start(out=q_raw1[:], in_=q_rows[:, :, QT : 2 * QT])
         nc.sync.dma_start(out=q_raw23[:], in_=q_rows[:, :, 2 * QT : 4 * QT])
-        nc.sync.dma_start(out=v_raw[:], in_=v[0].rearrange("(s r) e -> s r e", r=PACK))
 
         k_pack = sb.tile([P, N + N // PACK], U32, name="k_pack", align_bytes=64)
         k_codes = k_pack[:, 0:N].bitcast(FP8X4)
@@ -94,20 +93,38 @@ def tile_rows_a_silu_gate_kernel(tc, qT, kT, t, v, og, out):
             h, c = steps[i]
             return score_banks[c % 2] if h == 0 else score_banks[h + 1]
 
-        def scores(i):
+        def score_tile(i, r):
             h, c = steps[i]
             rows = slice(ROWS * h, ROWS * (h + 1))
+            cols = slice(P * r, P * (r + 1))
+            nc.tensor.matmul_mx(
+                out=bank_of(i)[:, QT * r : QT * (r + 1)],
+                lhsT=k_codes[rows, cols],
+                lhsT_scale=k_scales[rows, cols],
+                rhs=q_codes[c][rows, :].bitcast(FP8X4),
+                rhs_scale=q_scales[c][rows, :],
+                start=True,
+                stop=True,
+            )
+
+        def scores(i):
             for r in range(PACK):
-                cols = slice(P * r, P * (r + 1))
-                nc.tensor.matmul_mx(
-                    out=bank_of(i)[:, QT * r : QT * (r + 1)],
-                    lhsT=k_codes[rows, cols],
-                    lhsT_scale=k_scales[rows, cols],
-                    rhs=q_codes[c][rows, :].bitcast(FP8X4),
-                    rhs_scale=q_scales[c][rows, :],
-                    start=True,
-                    stop=True,
-                )
+                score_tile(i, r)
+
+        def skewed(j):
+            for r in range(2):
+                if j > CHUNKS:
+                    score_tile(j - 1, 2 + r)
+                if j < len(steps):
+                    score_tile(j, r)
+            if j > CHUNKS:
+                silu(j - 1)
+
+        def gate(c):
+            if c < 0:
+                nc.scalar.activation(out=gate_first[:], in_=og_first[:], func=ACT.Tanh, scale=0.5)
+            else:
+                nc.scalar.activation(out=gate_rest[c][:], in_=og_rest[:, :, c, :], func=ACT.Tanh, scale=0.5)
 
         def silu(i):
             nc.scalar.activation(out=p_sb[i][:], in_=bank_of(i)[:].rearrange("p (r n) -> p n r", r=PACK), func=ACT.Silu)
@@ -123,8 +140,10 @@ def tile_rows_a_silu_gate_kernel(tc, qT, kT, t, v, og, out):
         def group_of(i):
             return [n for n, g in enumerate(groups) if i in g][0]
 
-        def values(i):
+        def quantize_w(i):
             quantize(w_codes[i][:].bitcast(FP8X4), w_scales[i][:], w_bf[i][:].rearrange("p n j -> p (n j)"))
+
+        def values(i):
             n = group_of(i)
             slot = groups[n].index(i)
             nc.tensor.matmul_mx(
@@ -141,14 +160,14 @@ def tile_rows_a_silu_gate_kernel(tc, qT, kT, t, v, og, out):
             g = groups[n]
             h0, c0 = steps[g[0]]
             if h0 == 0:
-                gate = gate_first[:]
+                gate_ap = gate_first[:]
                 dst = out[0].rearrange("(c m) e -> m c e", m=QT)
             else:
-                gate = gate_rest[c0][:, h0 - 1 : h0 - 1 + len(g), :]
+                gate_ap = gate_rest[c0][:, h0 - 1 : h0 - 1 + len(g), :]
                 dst = out[h0 : h0 + len(g), QT * c0 : QT * (c0 + 1), :].rearrange("h m e -> m h e")
             nc.vector.scalar_tensor_tensor(
                 out=res[n][:].rearrange("p g e -> p (g e)"),
-                in0=gate.rearrange("p g e -> p (g e)"),
+                in0=gate_ap.rearrange("p g e -> p (g e)"),
                 scalar=1.0,
                 in1=y_banks[n % 3][:, 0 : E * len(g)],
                 op0=ALU.add,
@@ -159,8 +178,8 @@ def tile_rows_a_silu_gate_kernel(tc, qT, kT, t, v, og, out):
         nc.vector.tensor_copy(out=words_out(q_bf[0]), in_=words_in(q_raw[0]))
         k_src = k_raw[:].rearrange("p j (s r) -> p s r j", r=PACK)
         k_dst = k_bf[:].rearrange("p r s j -> p s r j")
-        quantize_q(0)
         nc.vector.tensor_copy(out=k_dst[:, 0:K_VECTOR, :, :], in_=k_src[:, 0:K_VECTOR, :, :])
+        quantize_q(0)
         nc.scalar.copy(out=k_dst[:, K_VECTOR:P, :, :], in_=k_src[:, K_VECTOR:P, :, :])
         nc.scalar.copy(out=words_out(q_bf[1]), in_=words_in(q_raw[1]))
         for r in range(PACK):
@@ -168,6 +187,7 @@ def tile_rows_a_silu_gate_kernel(tc, qT, kT, t, v, og, out):
             quantize(k_codes[0:ROWS, cols], k_scales[0:ROWS, cols], k_bf[:, r, :, :].rearrange("p s j -> p (s j)"))
         for h in range(1, H):
             nc.sync.dma_start(out=k_pack[ROWS * h : ROWS * (h + 1), :].bitcast(I32), in_=k_pack[0:ROWS, :].bitcast(I32))
+        nc.sync.dma_start(out=v_raw[:], in_=v[0].rearrange("(s r) e -> s r e", r=PACK))
         nc.sync.dma_start(out=og_first[:], in_=og[0].rearrange("(c m) e -> m c e", m=QT))
         nc.sync.dma_start(
             out=og_rest[:].rearrange("m h c e -> m (h c) e"),
@@ -183,31 +203,42 @@ def tile_rows_a_silu_gate_kernel(tc, qT, kT, t, v, og, out):
         quantize_q(2)
         scores(2)
         silu(2)
-        nc.scalar.activation(out=words_out(v_bf), in_=words_in(v_raw[:]), func=ACT.Copy, scale=1.0 / 32.0)
-
-        gates_after = {5: -1, 7: 0, 9: 1, 11: 2, 13: 3}
-        finish_after = {5: 0, 8: 1, 11: 2, 14: 3}
-        for i in range(len(steps)):
-            if i == 0:
-                weigh(0)
-                quantize_q(3)
-            j = i + LEAD
-            if j < len(steps):
-                scores(j)
-                silu(j)
-                if j in gates_after:
-                    c = gates_after[j]
-                    if c < 0:
-                        nc.scalar.activation(out=gate_first[:], in_=og_first[:], func=ACT.Tanh, scale=0.5)
-                    else:
-                        nc.scalar.activation(out=gate_rest[c][:], in_=og_rest[:, :, c, :], func=ACT.Tanh, scale=0.5)
-            if i > 0:
-                weigh(i)
-                if i == 1:
-                    quantize(v_codes[:].bitcast(FP8X4), v_scales[:], v_bf[:].rearrange("p e j -> p (e j)"))
+        weigh(0)
+        quantize_q(3)
+        scores(3)
+        silu(3)
+        for j in range(4, 13):
+            skewed(j)
+            if j == 6:
+                nc.scalar.activation(out=words_out(v_bf), in_=words_in(v_raw[:]), func=ACT.Copy, scale=1.0 / 32.0)
+            if j == 9:
+                gate(-1)
+        gate(0)
+        for i in range(1, 8):
+            weigh(i)
+            if i == 5:
+                quantize(v_codes[:].bitcast(FP8X4), v_scales[:], v_bf[:].rearrange("p e j -> p (e j)"))
+            quantize_w(i - 1)
+        for i in range(7):
+            values(i)
+        for j in range(13, 17):
+            skewed(j)
+            if j == 14:
+                gate(1)
+        gate(2)
+        gate(3)
+        for i in range(8, 16):
+            weigh(i)
+            quantize_w(i - 1)
+            if i == 10:
+                for m in groups[2]:
+                    values(m)
+            if i > 10:
                 values(i - 1)
-            if i in finish_after:
-                finish(finish_after[i], nc.sync)
-        values(len(steps) - 1)
-        finish(4, nc.sync)
-        finish(5, nc.scalar)
+            if i in (9, 10, 12):
+                finish({9: 0, 10: 1, 12: 2}[i], nc.sync)
+        quantize_w(15)
+        values(15)
+        finish(3, nc.sync)
+        finish(4, nc.scalar)
+        finish(5, nc.sync)

@@ -19,7 +19,7 @@ PACK = 4
 ROWS = 32
 QT = 128
 CHUNKS = NQ // QT
-K_VECTOR = 88
+K_VECTOR = 76
 LEAD = 3
 
 
@@ -37,18 +37,19 @@ def tile_rows_a_silu_gate_kernel(tc, qT, kT, t, v, og, out):
         q_raw0 = sb.tile([P, PACK, QT], F32, name="q_raw0")
         q_raw1 = sb.tile([P, PACK, QT], F32, name="q_raw1")
         q_raw23 = sb.tile([P, PACK, 2 * QT], F32, name="q_raw23")
-        q_raw = [q_raw0[:], q_raw1[:], q_raw23[:, :, 0:QT], q_raw23[:, :, QT : 2 * QT]]
+        q_raw = [q_raw0[:], q_raw1[:], q_raw23[:]]
         k_raw = sb.tile([ROWS, PACK, N], F32, name="k_raw")
         t_sb = sb.tile([P, PACK], F32, name="t_sb")
         v_raw = sb.tile([P, PACK, E], F32, name="v_raw")
         og_first = sb.tile([P, CHUNKS, E], F32, name="og_first")
         og_rest = sb.tile([P, H - 1, CHUNKS, E], F32, name="og_rest")
 
-        nc.sync.dma_start(out=q_raw0[:], in_=q_rows[:, :, 0:QT])
         nc.sync.dma_start(out=k_raw[:], in_=kT[0].rearrange("(p j) n -> p j n", j=PACK))
+        nc.sync.dma_start(out=q_raw0[:], in_=q_rows[:, :, 0:QT])
         nc.sync.dma_start(out=t_sb[:], in_=t.rearrange("(s r) o -> s (r o)", r=PACK))
         nc.sync.dma_start(out=q_raw1[:], in_=q_rows[:, :, QT : 2 * QT])
         nc.sync.dma_start(out=q_raw23[:], in_=q_rows[:, :, 2 * QT : 4 * QT])
+        nc.sync.dma_start(out=v_raw[:], in_=v[0].rearrange("(s r) e -> s r e", r=PACK))
 
         k_pack = sb.tile([P, N + N // PACK], U32, name="k_pack", align_bytes=64)
         k_codes = k_pack[:, 0:N].bitcast(FP8X4)
@@ -59,17 +60,19 @@ def tile_rows_a_silu_gate_kernel(tc, qT, kT, t, v, og, out):
         nc.vector.memset(warm[:, 0:1], 0.0)
         nc.scalar.activation(out=warm[:, 1:2], in_=warm[:, 0:1], func=ACT.Silu)
 
-        q_bf = [sb.tile([P, QT, PACK], BF16, name="q_bf%d" % c, align_bytes=64) for c in range(CHUNKS)]
-        q_codes = [sb.tile([P, QT], U32, name="q_codes%d" % c, align_bytes=64) for c in range(CHUNKS)]
-        q_scales = [sb.tile([P, QT], U8, name="q_scales%d" % c, align_bytes=64) for c in range(CHUNKS)]
+        widths = [QT, QT, 2 * QT]
+        q_bf = [sb.tile([P, n, PACK], BF16, name="q_bf%d" % c, align_bytes=64) for c, n in enumerate(widths)]
+        q_codes = sb.tile([P, NQ], U32, name="q_codes", align_bytes=64)
+        q_scales = sb.tile([P, NQ], U8, name="q_scales", align_bytes=64)
         k_bf = sb.tile([ROWS, PACK, P, PACK], BF16, name="k_bf", align_bytes=64)
         v_bf = sb.tile([P, E, PACK], BF16, name="v_bf", align_bytes=64)
         v_codes = sb.tile([P, E], U32, name="v_codes", align_bytes=64)
         v_scales = sb.tile([P, E], U8, name="v_scales", align_bytes=64)
-        p_sb = [sb.tile([P, QT, PACK], F32, name="p%d" % i) for i in range(len(steps))]
-        w_bf = [sb.tile([P, QT, PACK], BF16, name="w_bf%d" % i, align_bytes=64) for i in range(len(steps))]
-        w_codes = [sb.tile([P, QT], U32, name="w_codes%d" % i, align_bytes=64) for i in range(len(steps))]
-        w_scales = [sb.tile([P, QT], U8, name="w_scales%d" % i, align_bytes=64) for i in range(len(steps))]
+        STEP = QT * PACK
+        p_sb = sb.tile([P, len(steps) * STEP], F32, name="p_sb")
+        w_bf = sb.tile([P, 14 * STEP], BF16, name="w_bf", align_bytes=64)
+        w_codes = sb.tile([P, len(steps) * QT], U32, name="w_codes", align_bytes=64)
+        w_scales = sb.tile([P, len(steps) * QT], U8, name="w_scales", align_bytes=64)
         gate_first = sb.tile([P, CHUNKS, E], F32, name="gate_first")
         gate_rest = [sb.tile([P, H - 1, E], F32, name="gate_rest%d" % c) for c in range(CHUNKS)]
         res = [sb.tile([P, len(g), E], F32, name="res%d" % n) for n, g in enumerate(groups)]
@@ -87,7 +90,8 @@ def tile_rows_a_silu_gate_kernel(tc, qT, kT, t, v, og, out):
             nc.vector.quantize_mx(out=codes, scales=scales, in_=values)
 
         def quantize_q(c):
-            quantize(q_codes[c][:].bitcast(FP8X4), q_scales[c][:], q_bf[c][:].rearrange("p n j -> p (n j)"))
+            cols = slice(QT * c, QT * c + widths[c])
+            quantize(q_codes[:, cols].bitcast(FP8X4), q_scales[:, cols], q_bf[c][:].rearrange("p n j -> p (n j)"))
 
         def bank_of(i):
             h, c = steps[i]
@@ -101,8 +105,8 @@ def tile_rows_a_silu_gate_kernel(tc, qT, kT, t, v, og, out):
                 out=bank_of(i)[:, QT * r : QT * (r + 1)],
                 lhsT=k_codes[rows, cols],
                 lhsT_scale=k_scales[rows, cols],
-                rhs=q_codes[c][rows, :].bitcast(FP8X4),
-                rhs_scale=q_scales[c][rows, :],
+                rhs=q_codes[rows, QT * c : QT * (c + 1)].bitcast(FP8X4),
+                rhs_scale=q_scales[rows, QT * c : QT * (c + 1)],
                 start=True,
                 stop=True,
             )
@@ -127,29 +131,39 @@ def tile_rows_a_silu_gate_kernel(tc, qT, kT, t, v, og, out):
                 nc.scalar.activation(out=gate_rest[c][:], in_=og_rest[:, :, c, :], func=ACT.Tanh, scale=0.5)
 
         def silu(i):
-            nc.scalar.activation(out=p_sb[i][:], in_=bank_of(i)[:].rearrange("p (r n) -> p n r", r=PACK), func=ACT.Silu)
+            nc.scalar.activation(
+                out=p_sb[:, STEP * i : STEP * (i + 1)].rearrange("p (n r) -> p n r", r=PACK),
+                in_=bank_of(i)[:].rearrange("p (r n) -> p n r", r=PACK),
+                func=ACT.Silu,
+            )
 
-        def weigh(i):
-            nc.vector.tensor_tensor(
-                out=w_bf[i][:],
-                in0=p_sb[i][:],
-                in1=t_sb[:, 0:PACK].unsqueeze(1).to_broadcast([P, QT, PACK]),
+        def w_cols(i, count):
+            first = i if i < 14 else i - 4
+            return slice(STEP * first, STEP * (first + count))
+
+        def weigh(i, count, engine=nc.vector):
+            cols = slice(STEP * i, STEP * (i + count))
+            engine.tensor_tensor(
+                out=w_bf[:, w_cols(i, count)].rearrange("p (n r) -> p n r", r=PACK),
+                in0=p_sb[:, cols].rearrange("p (n r) -> p n r", r=PACK),
+                in1=t_sb[:, 0:PACK].unsqueeze(1).to_broadcast([P, QT * count, PACK]),
                 op=ALU.mult,
             )
 
         def group_of(i):
             return [n for n, g in enumerate(groups) if i in g][0]
 
-        def quantize_w(i):
-            quantize(w_codes[i][:].bitcast(FP8X4), w_scales[i][:], w_bf[i][:].rearrange("p n j -> p (n j)"))
+        def quantize_w(i, count):
+            cols = slice(QT * i, QT * (i + count))
+            quantize(w_codes[:, cols].bitcast(FP8X4), w_scales[:, cols], w_bf[:, w_cols(i, count)])
 
         def values(i):
             n = group_of(i)
             slot = groups[n].index(i)
             nc.tensor.matmul_mx(
                 out=y_banks[n % 3][:, E * slot : E * (slot + 1)],
-                lhsT=w_codes[i][:].bitcast(FP8X4),
-                lhsT_scale=w_scales[i][:],
+                lhsT=w_codes[:, QT * i : QT * (i + 1)].bitcast(FP8X4),
+                lhsT_scale=w_scales[:, QT * i : QT * (i + 1)],
                 rhs=v_codes[:].bitcast(FP8X4),
                 rhs_scale=v_scales[:],
                 start=True,
@@ -175,19 +189,26 @@ def tile_rows_a_silu_gate_kernel(tc, qT, kT, t, v, og, out):
             )
             queue.dma_start(out=dst, in_=res[n][:])
 
-        nc.vector.tensor_copy(out=words_out(q_bf[0]), in_=words_in(q_raw[0]))
+        def quantize_k(r):
+            cols = slice(P * r, P * (r + 1))
+            quantize(k_codes[0:ROWS, cols], k_scales[0:ROWS, cols], k_bf[:, r, :, :].rearrange("p s j -> p (s j)"))
+
+        def group_values(n):
+            for i in groups[n]:
+                values(i)
+
         k_src = k_raw[:].rearrange("p j (s r) -> p s r j", r=PACK)
         k_dst = k_bf[:].rearrange("p r s j -> p s r j")
         nc.vector.tensor_copy(out=k_dst[:, 0:K_VECTOR, :, :], in_=k_src[:, 0:K_VECTOR, :, :])
-        quantize_q(0)
         nc.scalar.copy(out=k_dst[:, K_VECTOR:P, :, :], in_=k_src[:, K_VECTOR:P, :, :])
+        nc.vector.tensor_copy(out=words_out(q_bf[0]), in_=words_in(q_raw[0]))
         nc.scalar.copy(out=words_out(q_bf[1]), in_=words_in(q_raw[1]))
-        for r in range(PACK):
-            cols = slice(P * r, P * (r + 1))
-            quantize(k_codes[0:ROWS, cols], k_scales[0:ROWS, cols], k_bf[:, r, :, :].rearrange("p s j -> p (s j)"))
+        quantize_k(0)
+        quantize_q(0)
+        for r in range(1, PACK):
+            quantize_k(r)
         for h in range(1, H):
             nc.sync.dma_start(out=k_pack[ROWS * h : ROWS * (h + 1), :].bitcast(I32), in_=k_pack[0:ROWS, :].bitcast(I32))
-        nc.sync.dma_start(out=v_raw[:], in_=v[0].rearrange("(s r) e -> s r e", r=PACK))
         nc.sync.dma_start(out=og_first[:], in_=og[0].rearrange("(c m) e -> m c e", m=QT))
         nc.sync.dma_start(
             out=og_rest[:].rearrange("m h c e -> m (h c) e"),
@@ -195,49 +216,39 @@ def tile_rows_a_silu_gate_kernel(tc, qT, kT, t, v, og, out):
         )
         quantize_q(1)
         nc.vector.tensor_copy(out=words_out(q_bf[2]), in_=words_in(q_raw[2]))
-        scores(0)
-        silu(0)
-        scores(1)
-        silu(1)
-        nc.scalar.copy(out=words_out(q_bf[3]), in_=words_in(q_raw[3]))
         quantize_q(2)
-        scores(2)
-        silu(2)
-        weigh(0)
-        quantize_q(3)
-        scores(3)
-        silu(3)
-        for j in range(4, 13):
+        for i in range(CHUNKS):
+            scores(i)
+            silu(i)
+        for j in range(4, 17):
             skewed(j)
-            if j == 6:
-                nc.scalar.activation(out=words_out(v_bf), in_=words_in(v_raw[:]), func=ACT.Copy, scale=1.0 / 32.0)
-            if j == 9:
-                gate(-1)
-        gate(0)
-        for i in range(1, 8):
-            weigh(i)
-            if i == 5:
-                quantize(v_codes[:].bitcast(FP8X4), v_scales[:], v_bf[:].rearrange("p e j -> p (e j)"))
-            quantize_w(i - 1)
-        for i in range(7):
-            values(i)
-        for j in range(13, 17):
-            skewed(j)
-            if j == 14:
-                gate(1)
+            if j >= 14:
+                gate(j - 15)
         gate(2)
         gate(3)
-        for i in range(8, 16):
-            weigh(i)
-            quantize_w(i - 1)
-            if i == 10:
-                for m in groups[2]:
-                    values(m)
-            if i > 10:
-                values(i - 1)
-            if i in (9, 10, 12):
-                finish({9: 0, 10: 1, 12: 2}[i], nc.sync)
-        quantize_w(15)
+        weigh(0, 1)
+        weigh(1, 1)
+        nc.vector.tensor_scalar(
+            out=v_bf[:], in0=v_raw[:].rearrange("p r e -> p e r"), scalar1=1.0 / 32.0, scalar2=None, op0=ALU.mult
+        )
+        quantize_w(0, 2)
+        quantize(v_codes[:].bitcast(FP8X4), v_scales[:], v_bf[:].rearrange("p e j -> p (e j)"))
+        weigh(2, 2)
+        for i in range(4, 14, 2):
+            weigh(i, 2)
+            quantize_w(i - 2, 2)
+        for n in range(3):
+            group_values(n)
+        weigh(14, 1, nc.gpsimd)
+        for n in range(3):
+            finish(n, nc.sync)
+        quantize_w(12, 2)
+        group_values(3)
+        values(13)
+        weigh(15, 1)
+        quantize_w(14, 1)
+        values(14)
+        quantize_w(15, 1)
         values(15)
         finish(3, nc.sync)
         finish(4, nc.scalar)

@@ -19,14 +19,14 @@ PACK = 4
 ROWS = 32
 QT = 128
 CHUNKS = NQ // QT
-K_VECTOR = 76
+K_VECTOR = 86
 LEAD = 3
 
 
 def tile_rows_a_silu_gate_kernel(tc, qT, kT, t, v, og, out):
     nc = tc.nc
-    steps = [(0, c) for c in range(CHUNKS)] + [(h, c) for c in range(CHUNKS) for h in range(1, H)]
-    groups = [[0, 1, 2, 3], [4, 5, 6], [7, 8, 9], [10, 11, 12], [13, 14], [15]]
+    steps = [(0, c) for c in range(CHUNKS)] + [(h, c) for c in range(CHUNKS) for h in (2, 3, 1)]
+    groups = [[0, 1, 2, 3], [4, 7, 5, 8], [6, 9], [10, 13], [11, 14], [12, 15]]
 
     with ExitStack() as ctx:
         sb = ctx.enter_context(tc.tile_pool(name="sb", bufs=1))
@@ -34,22 +34,17 @@ def tile_rows_a_silu_gate_kernel(tc, qT, kT, t, v, og, out):
         ctx.enter_context(tc.manual_schedule())
 
         q_rows = qT.rearrange("h (p j) n -> (h p) j n", j=PACK)
-        q_raw0 = sb.tile([P, PACK, QT], F32, name="q_raw0")
-        q_raw1 = sb.tile([P, PACK, QT], F32, name="q_raw1")
-        q_raw23 = sb.tile([P, PACK, 2 * QT], F32, name="q_raw23")
-        q_raw = [q_raw0[:], q_raw1[:], q_raw23[:]]
+        q_raw = [sb.tile([P, PACK, 2 * QT], F32, name="q_raw%d" % b) for b in range(2)]
         k_raw = sb.tile([ROWS, PACK, N], F32, name="k_raw")
         t_sb = sb.tile([P, PACK], F32, name="t_sb")
         v_raw = sb.tile([P, PACK, E], F32, name="v_raw")
-        og_first = sb.tile([P, CHUNKS, E], F32, name="og_first")
-        og_rest = sb.tile([P, H - 1, CHUNKS, E], F32, name="og_rest")
+        og_first = sb.tile([P, 2, 2 * E], F32, name="og_first")
+        og_rest = sb.tile([P, H - 1, 2, 2 * E], F32, name="og_rest")
 
         nc.sync.dma_start(out=k_raw[:], in_=kT[0].rearrange("(p j) n -> p j n", j=PACK))
-        nc.sync.dma_start(out=q_raw0[:], in_=q_rows[:, :, 0:QT])
-        nc.sync.dma_start(out=t_sb[:], in_=t.rearrange("(s r) o -> s (r o)", r=PACK))
-        nc.sync.dma_start(out=q_raw1[:], in_=q_rows[:, :, QT : 2 * QT])
-        nc.sync.dma_start(out=q_raw23[:], in_=q_rows[:, :, 2 * QT : 4 * QT])
-        nc.sync.dma_start(out=v_raw[:], in_=v[0].rearrange("(s r) e -> s r e", r=PACK))
+        nc.scalar.dma_start(out=t_sb[:], in_=t.rearrange("(s r) o -> s (r o)", r=PACK))
+        for b in range(2):
+            nc.sync.dma_start(out=q_raw[b][:], in_=q_rows[:, :, 2 * QT * b : 2 * QT * (b + 1)])
 
         k_pack = sb.tile([P, N + N // PACK], U32, name="k_pack", align_bytes=64)
         k_codes = k_pack[:, 0:N].bitcast(FP8X4)
@@ -60,7 +55,7 @@ def tile_rows_a_silu_gate_kernel(tc, qT, kT, t, v, og, out):
         nc.vector.memset(warm[:, 0:1], 0.0)
         nc.scalar.activation(out=warm[:, 1:2], in_=warm[:, 0:1], func=ACT.Silu)
 
-        widths = [QT, QT, 2 * QT]
+        widths = [QT, QT, QT, QT]
         q_bf = [sb.tile([P, n, PACK], BF16, name="q_bf%d" % c, align_bytes=64) for c, n in enumerate(widths)]
         q_codes = sb.tile([P, NQ], U32, name="q_codes", align_bytes=64)
         q_scales = sb.tile([P, NQ], U8, name="q_scales", align_bytes=64)
@@ -73,8 +68,8 @@ def tile_rows_a_silu_gate_kernel(tc, qT, kT, t, v, og, out):
         w_bf = sb.tile([P, 14 * STEP], BF16, name="w_bf", align_bytes=64)
         w_codes = sb.tile([P, len(steps) * QT], U32, name="w_codes", align_bytes=64)
         w_scales = sb.tile([P, len(steps) * QT], U8, name="w_scales", align_bytes=64)
-        gate_first = sb.tile([P, CHUNKS, E], F32, name="gate_first")
-        gate_rest = [sb.tile([P, H - 1, E], F32, name="gate_rest%d" % c) for c in range(CHUNKS)]
+        gate_first = sb.tile([P, 2, 2 * E], F32, name="gate_first")
+        gate_rest = [sb.tile([P, H - 1, 2 * E], F32, name="gate_rest%d" % b) for b in range(2)]
         res = [sb.tile([P, len(g), E], F32, name="res%d" % n) for n, g in enumerate(groups)]
 
         score_banks = [ps.tile([P, PACK * QT], F32, name="score%d" % b) for b in range(H + 1)]
@@ -83,8 +78,8 @@ def tile_rows_a_silu_gate_kernel(tc, qT, kT, t, v, og, out):
         def words_out(tile):
             return tile[:].rearrange("p (c i) j -> p c j i", i=4)
 
-        def words_in(raw):
-            return raw.rearrange("p j (c i) -> p c j i", i=4)
+        def words_in(raw, u):
+            return raw[:].rearrange("p j (c i u) -> p u c j i", i=4, u=2)[:, u, :, :, :]
 
         def quantize(codes, scales, values):
             nc.vector.quantize_mx(out=codes, scales=scales, in_=values)
@@ -124,11 +119,8 @@ def tile_rows_a_silu_gate_kernel(tc, qT, kT, t, v, og, out):
             if j > CHUNKS:
                 silu(j - 1)
 
-        def gate(c):
-            if c < 0:
-                nc.scalar.activation(out=gate_first[:], in_=og_first[:], func=ACT.Tanh, scale=0.5)
-            else:
-                nc.scalar.activation(out=gate_rest[c][:], in_=og_rest[:, :, c, :], func=ACT.Tanh, scale=0.5)
+        def gate(dst, src):
+            nc.scalar.activation(out=dst, in_=src, func=ACT.Tanh, scale=0.5)
 
         def silu(i):
             nc.scalar.activation(
@@ -170,24 +162,34 @@ def tile_rows_a_silu_gate_kernel(tc, qT, kT, t, v, og, out):
                 stop=True,
             )
 
-        def finish(n, queue):
-            g = groups[n]
-            h0, c0 = steps[g[0]]
+        def gated(n, first, last):
+            h0, c0 = steps[groups[n][0]]
             if h0 == 0:
-                gate_ap = gate_first[:]
-                dst = out[0].rearrange("(c m) e -> m c e", m=QT)
+                gate_ap = gate_first[:].rearrange("p b x -> p (b x)")
             else:
-                gate_ap = gate_rest[c0][:, h0 - 1 : h0 - 1 + len(g), :]
-                dst = out[h0 : h0 + len(g), QT * c0 : QT * (c0 + 1), :].rearrange("h m e -> m h e")
+                gate_ap = gate_rest[c0 // 2][:, h0 - 1 :, :].rearrange("p h x -> p (h x)")
+            cols = slice(E * first, E * last)
             nc.vector.scalar_tensor_tensor(
-                out=res[n][:].rearrange("p g e -> p (g e)"),
-                in0=gate_ap.rearrange("p g e -> p (g e)"),
+                out=res[n][:].rearrange("p g e -> p (g e)")[:, cols],
+                in0=gate_ap[:, cols],
                 scalar=1.0,
-                in1=y_banks[n % 3][:, 0 : E * len(g)],
+                in1=y_banks[n % 3][:, cols],
                 op0=ALU.add,
                 op1=ALU.mult,
             )
-            queue.dma_start(out=dst, in_=res[n][:])
+
+        def store(n, queue):
+            h0, c0 = steps[groups[n][0]]
+            if h0 == 0:
+                dst = out[0].rearrange("(b m u) e -> m b (u e)", m=QT, u=2)
+            else:
+                rows = slice(2 * QT * (c0 // 2), 2 * QT * (c0 // 2 + 1))
+                dst = out[h0 : h0 + len(groups[n]) // 2, rows, :].rearrange("h (m u) e -> m h (u e)", u=2)
+            queue.dma_start(out=dst, in_=res[n][:].rearrange("p (b u) e -> p b (u e)", u=2))
+
+        def finish(n, queue):
+            gated(n, 0, len(groups[n]))
+            store(n, queue)
 
         def quantize_k(r):
             cols = slice(P * r, P * (r + 1))
@@ -201,39 +203,45 @@ def tile_rows_a_silu_gate_kernel(tc, qT, kT, t, v, og, out):
         k_dst = k_bf[:].rearrange("p r s j -> p s r j")
         nc.vector.tensor_copy(out=k_dst[:, 0:K_VECTOR, :, :], in_=k_src[:, 0:K_VECTOR, :, :])
         nc.scalar.copy(out=k_dst[:, K_VECTOR:P, :, :], in_=k_src[:, K_VECTOR:P, :, :])
-        nc.vector.tensor_copy(out=words_out(q_bf[0]), in_=words_in(q_raw[0]))
-        nc.scalar.copy(out=words_out(q_bf[1]), in_=words_in(q_raw[1]))
         quantize_k(0)
+        quantize_k(1)
+        nc.vector.tensor_copy(out=words_out(q_bf[0]), in_=words_in(q_raw[0], 0))
+        nc.scalar.copy(out=words_out(q_bf[1]), in_=words_in(q_raw[0], 1))
+        quantize_k(2)
         quantize_q(0)
-        for r in range(1, PACK):
-            quantize_k(r)
-        for h in range(1, H):
+        quantize_k(3)
+        for h in (2, 3, 1):
             nc.sync.dma_start(out=k_pack[ROWS * h : ROWS * (h + 1), :].bitcast(I32), in_=k_pack[0:ROWS, :].bitcast(I32))
-        nc.sync.dma_start(out=og_first[:], in_=og[0].rearrange("(c m) e -> m c e", m=QT))
+        nc.sync.dma_start(out=v_raw[:], in_=v[0].rearrange("(s r) e -> s r e", r=PACK))
+        nc.sync.dma_start(out=og_first[:], in_=og[0].rearrange("(b m u) e -> m b (u e)", m=QT, u=2))
         nc.sync.dma_start(
-            out=og_rest[:].rearrange("m h c e -> m (h c) e"),
-            in_=og[1:H].rearrange("h (c m) e -> m (h c) e", m=QT),
+            out=og_rest[:].rearrange("m h b x -> m (h b) x"),
+            in_=og[1:H].rearrange("h (b m u) e -> m (h b) (u e)", m=QT, u=2),
         )
         quantize_q(1)
-        nc.vector.tensor_copy(out=words_out(q_bf[2]), in_=words_in(q_raw[2]))
+        for u in range(2):
+            nc.vector.tensor_copy(out=words_out(q_bf[2 + u]), in_=words_in(q_raw[1], u))
         quantize_q(2)
+        quantize_q(3)
         for i in range(CHUNKS):
             scores(i)
             silu(i)
         for j in range(4, 17):
             skewed(j)
-            if j >= 14:
-                gate(j - 15)
-        gate(2)
-        gate(3)
-        weigh(0, 1)
-        weigh(1, 1)
+            if j == 14:
+                gate(gate_first[:], og_first[:])
+            if j == 15:
+                gate(gate_rest[0][:, 1:3, :], og_rest[:, 1:3, 0, :])
+        gate(gate_rest[0][:, 0, :], og_rest[:, 0, 0, :])
+        gate(gate_rest[1][:], og_rest[:, :, 1, :])
+        for i in range(3):
+            weigh(i, 1)
+        quantize_w(0, 2)
         nc.vector.tensor_scalar(
             out=v_bf[:], in0=v_raw[:].rearrange("p r e -> p e r"), scalar1=1.0 / 32.0, scalar2=None, op0=ALU.mult
         )
-        quantize_w(0, 2)
+        weigh(3, 1)
         quantize(v_codes[:].bitcast(FP8X4), v_scales[:], v_bf[:].rearrange("p e j -> p (e j)"))
-        weigh(2, 2)
         for i in range(4, 14, 2):
             weigh(i, 2)
             quantize_w(i - 2, 2)
@@ -243,13 +251,15 @@ def tile_rows_a_silu_gate_kernel(tc, qT, kT, t, v, og, out):
         for n in range(3):
             finish(n, nc.sync)
         quantize_w(12, 2)
-        group_values(3)
-        values(13)
+        for i in (12, 10, 13, 11):
+            values(i)
         weigh(15, 1)
         quantize_w(14, 1)
         values(14)
+        gated(5, 0, 1)
         quantize_w(15, 1)
         values(15)
         finish(3, nc.sync)
         finish(4, nc.scalar)
-        finish(5, nc.sync)
+        gated(5, 1, 2)
+        store(5, nc.sync)

@@ -51,10 +51,6 @@ def tile_rows_a_silu_gate_kernel(tc, qT, kT, t, v, og, out):
         k_scales = k_pack[:, N : N + N // PACK].bitcast(U8)
         nc.vector.memset(k_pack[0:ROWS, N : N + N // PACK].bitcast(I32), 0)
 
-        warm = sb.tile([P, 2], F32, name="warm")
-        nc.vector.memset(warm[:, 0:1], 0.0)
-        nc.scalar.activation(out=warm[:, 1:2], in_=warm[:, 0:1], func=ACT.Silu)
-
         widths = [QT, QT, QT, QT]
         q_bf = [sb.tile([P, n, PACK], BF16, name="q_bf%d" % c, align_bytes=64) for c, n in enumerate(widths)]
         q_codes = sb.tile([P, NQ], U32, name="q_codes", align_bytes=64)

from contextlib import ExitStack

import concourse.mybir as mybir

H, D, NQ, N, E = 4, 128, 512, 512, 128
FLOPS = 2 * H * NQ * N * (D + E)

F32 = mybir.dt.float32
BF16 = mybir.dt.bfloat16
U32 = mybir.dt.uint32
I32 = mybir.dt.int32
U8 = mybir.dt.uint8
FP8X4 = mybir.dt.float8_e4m3fn_x4
ACT = mybir.ActivationFunctionType
ALU = mybir.AluOpType

P = 128
PACK = 4
ROWS = 32
QT = 128
CHUNKS = NQ // QT
K_VECTOR = 86
LEAD = 3


def tile_rows_a_silu_gate_kernel(tc, qT, kT, t, v, og, out):
    nc = tc.nc
    steps = [(0, c) for c in range(CHUNKS)] + [(h, c) for c in range(CHUNKS) for h in (2, 3, 1)]
    groups = [[0, 1, 2, 3], [4, 7, 5, 8], [6, 9], [10, 13], [11, 14], [12, 15]]

    with ExitStack() as ctx:
        sb = ctx.enter_context(tc.tile_pool(name="sb", bufs=1))
        ps = ctx.enter_context(tc.psum_pool(name="ps", bufs=1))
        ctx.enter_context(tc.manual_schedule())

        q_rows = qT.rearrange("h (p j) n -> (h p) j n", j=PACK)
        q_raw = [sb.tile([P, PACK, 2 * QT], F32, name="q_raw%d" % b) for b in range(2)]
        k_raw = sb.tile([ROWS, PACK, N], F32, name="k_raw")
        t_sb = sb.tile([P, PACK], F32, name="t_sb")
        v_raw = sb.tile([P, PACK, E], F32, name="v_raw")
        og_first = sb.tile([P, 2, 2 * E], F32, name="og_first")
        og_rest = sb.tile([P, H - 1, 2, 2 * E], F32, name="og_rest")

        nc.sync.dma_start(out=k_raw[:], in_=kT[0].rearrange("(p j) n -> p j n", j=PACK))
        nc.scalar.dma_start(out=t_sb[:], in_=t.rearrange("(s r) o -> s (r o)", r=PACK))
        for b in range(2):
            nc.sync.dma_start(out=q_raw[b][:], in_=q_rows[:, :, 2 * QT * b : 2 * QT * (b + 1)])

        k_pack = sb.tile([P, N + N // PACK], U32, name="k_pack", align_bytes=64)
        k_codes = k_pack[:, 0:N].bitcast(FP8X4)
        k_scales = k_pack[:, N : N + N // PACK].bitcast(U8)
        nc.vector.memset(k_pack[0:ROWS, N : N + N // PACK].bitcast(I32), 0)

        widths = [QT, QT, QT, QT]
        q_bf = [sb.tile([P, n, PACK], BF16, name="q_bf%d" % c, align_bytes=64) for c, n in enumerate(widths)]
        q_codes = sb.tile([P, NQ], U32, name="q_codes", align_bytes=64)
        q_scales = sb.tile([P, NQ], U8, name="q_scales", align_bytes=64)
        k_bf = sb.tile([ROWS, PACK, P, PACK], BF16, name="k_bf", align_bytes=64)
        v_bf = sb.tile([P, E, PACK], BF16, name="v_bf", align_bytes=64)
        v_codes = sb.tile([P, E], U32, name="v_codes", align_bytes=64)
        v_scales = sb.tile([P, E], U8, name="v_scales", align_bytes=64)
        STEP = QT * PACK
        p_sb = sb.tile([P, len(steps) * STEP], F32, name="p_sb")
        w_bf = sb.tile([P, 14 * STEP], BF16, name="w_bf", align_bytes=64)
        w_codes = sb.tile([P, len(steps) * QT], U32, name="w_codes", align_bytes=64)
        w_scales = sb.tile([P, len(steps) * QT], U8, name="w_scales", align_bytes=64)
        gate_first = sb.tile([P, 2, 2 * E], F32, name="gate_first")
        gate_rest = [sb.tile([P, H - 1, 2 * E], F32, name="gate_rest%d" % b) for b in range(2)]
        res = [sb.tile([P, len(g), E], F32, name="res%d" % n) for n, g in enumerate(groups)]

        score_banks = [ps.tile([P, PACK * QT], F32, name="score%d" % b) for b in range(H + 1)]
        y_banks = [ps.tile([P, PACK * E], F32, name="y%d" % b) for b in range(3)]

        def words_out(tile):
            return tile[:].rearrange("p (c i) j -> p c j i", i=4)

        def words_in(raw, u):
            return raw[:].rearrange("p j (c i u) -> p u c j i", i=4, u=2)[:, u, :, :, :]

        def quantize(codes, scales, values):
            nc.vector.quantize_mx(out=codes, scales=scales, in_=values)

        def quantize_q(c):
            cols = slice(QT * c, QT * c + widths[c])
            quantize(q_codes[:, cols].bitcast(FP8X4), q_scales[:, cols], q_bf[c][:].rearrange("p n j -> p (n j)"))

        def bank_of(i):
            h, c = steps[i]
            return score_banks[c % 2] if h == 0 else score_banks[h + 1]

        def score_tile(i, r):
            h, c = steps[i]
            rows = slice(ROWS * h, ROWS * (h + 1))
            cols = slice(P * r, P * (r + 1))
            nc.tensor.matmul_mx(
                out=bank_of(i)[:, QT * r : QT * (r + 1)],
                lhsT=k_codes[rows, cols],
                lhsT_scale=k_scales[rows, cols],
                rhs=q_codes[rows, QT * c : QT * (c + 1)].bitcast(FP8X4),
                rhs_scale=q_scales[rows, QT * c : QT * (c + 1)],
                start=True,
                stop=True,
            )

        def scores(i):
            for r in range(PACK):
                score_tile(i, r)

        def skewed(j):
            for r in range(2):
                if j > CHUNKS:
                    score_tile(j - 1, 2 + r)
                if j < len(steps):
                    score_tile(j, r)
            if j > CHUNKS:
                silu(j - 1)

        def gate(dst, src):
            nc.scalar.activation(out=dst, in_=src, func=ACT.Tanh, scale=0.5)

        def silu(i):
            nc.scalar.activation(
                out=p_sb[:, STEP * i : STEP * (i + 1)].rearrange("p (n r) -> p n r", r=PACK),
                in_=bank_of(i)[:].rearrange("p (r n) -> p n r", r=PACK),
                func=ACT.Silu,
            )

        def w_cols(i, count):
            first = i if i < 14 else i - 4
            return slice(STEP * first, STEP * (first + count))

        def weigh(i, count, engine=nc.vector):
            cols = slice(STEP * i, STEP * (i + count))
            engine.tensor_tensor(
                out=w_bf[:, w_cols(i, count)].rearrange("p (n r) -> p n r", r=PACK),
                in0=p_sb[:, cols].rearrange("p (n r) -> p n r", r=PACK),
                in1=t_sb[:, 0:PACK].unsqueeze(1).to_broadcast([P, QT * count, PACK]),
                op=ALU.mult,
            )

        def group_of(i):
            return [n for n, g in enumerate(groups) if i in g][0]

        def quantize_w(i, count):
            cols = slice(QT * i, QT * (i + count))
            quantize(w_codes[:, cols].bitcast(FP8X4), w_scales[:, cols], w_bf[:, w_cols(i, count)])

        def values(i):
            n = group_of(i)
            slot = groups[n].index(i)
            nc.tensor.matmul_mx(
                out=y_banks[n % 3][:, E * slot : E * (slot + 1)],
                lhsT=w_codes[:, QT * i : QT * (i + 1)].bitcast(FP8X4),
                lhsT_scale=w_scales[:, QT * i : QT * (i + 1)],
                rhs=v_codes[:].bitcast(FP8X4),
                rhs_scale=v_scales[:],
                start=True,
                stop=True,
            )

        def gated(n, first, last):
            h0, c0 = steps[groups[n][0]]
            if h0 == 0:
                gate_ap = gate_first[:].rearrange("p b x -> p (b x)")
            else:
                gate_ap = gate_rest[c0 // 2][:, h0 - 1 :, :].rearrange("p h x -> p (h x)")
            cols = slice(E * first, E * last)
            nc.vector.scalar_tensor_tensor(
                out=res[n][:].rearrange("p g e -> p (g e)")[:, cols],
                in0=gate_ap[:, cols],
                scalar=1.0,
                in1=y_banks[n % 3][:, cols],
                op0=ALU.add,
                op1=ALU.mult,
            )

        def store(n, queue):
            h0, c0 = steps[groups[n][0]]
            if h0 == 0:
                dst = out[0].rearrange("(b m u) e -> m b (u e)", m=QT, u=2)
            else:
                rows = slice(2 * QT * (c0 // 2), 2 * QT * (c0 // 2 + 1))
                dst = out[h0 : h0 + len(groups[n]) // 2, rows, :].rearrange("h (m u) e -> m h (u e)", u=2)
            queue.dma_start(out=dst, in_=res[n][:].rearrange("p (b u) e -> p b (u e)", u=2))

        def finish(n, queue):
            gated(n, 0, len(groups[n]))
            store(n, queue)

        def quantize_k(r):
            cols = slice(P * r, P * (r + 1))
            quantize(k_codes[0:ROWS, cols], k_scales[0:ROWS, cols], k_bf[:, r, :, :].rearrange("p s j -> p (s j)"))

        def group_values(n):
            for i in groups[n]:
                values(i)

        k_src = k_raw[:].rearrange("p j (s r) -> p s r j", r=PACK)
        k_dst = k_bf[:].rearrange("p r s j -> p s r j")
        nc.vector.tensor_copy(out=k_dst[:, 0:K_VECTOR, :, :], in_=k_src[:, 0:K_VECTOR, :, :])
        nc.scalar.copy(out=k_dst[:, K_VECTOR:P, :, :], in_=k_src[:, K_VECTOR:P, :, :])
        quantize_k(0)
        quantize_k(1)
        nc.vector.tensor_copy(out=words_out(q_bf[0]), in_=words_in(q_raw[0], 0))
        nc.scalar.copy(out=words_out(q_bf[1]), in_=words_in(q_raw[0], 1))
        quantize_k(2)
        quantize_q(0)
        quantize_k(3)
        for h in (2, 3, 1):
            nc.sync.dma_start(out=k_pack[ROWS * h : ROWS * (h + 1), :].bitcast(I32), in_=k_pack[0:ROWS, :].bitcast(I32))
        nc.sync.dma_start(out=v_raw[:], in_=v[0].rearrange("(s r) e -> s r e", r=PACK))
        nc.sync.dma_start(out=og_first[:], in_=og[0].rearrange("(b m u) e -> m b (u e)", m=QT, u=2))
        nc.sync.dma_start(
            out=og_rest[:].rearrange("m h b x -> m (h b) x"),
            in_=og[1:H].rearrange("h (b m u) e -> m (h b) (u e)", m=QT, u=2),
        )
        quantize_q(1)
        for u in range(2):
            nc.vector.tensor_copy(out=words_out(q_bf[2 + u]), in_=words_in(q_raw[1], u))
        quantize_q(2)
        quantize_q(3)
        for i in range(CHUNKS):
            scores(i)
            silu(i)
        for j in range(4, 17):
            skewed(j)
            if j == 14:
                gate(gate_first[:], og_first[:])
            if j == 15:
                gate(gate_rest[0][:, 1:3, :], og_rest[:, 1:3, 0, :])
        gate(gate_rest[0][:, 0, :], og_rest[:, 0, 0, :])
        gate(gate_rest[1][:], og_rest[:, :, 1, :])
        for i in range(3):
            weigh(i, 1)
        quantize_w(0, 2)
        nc.vector.tensor_scalar(
            out=v_bf[:], in0=v_raw[:].rearrange("p r e -> p e r"), scalar1=1.0 / 32.0, scalar2=None, op0=ALU.mult
        )
        weigh(3, 1)
        quantize(v_codes[:].bitcast(FP8X4), v_scales[:], v_bf[:].rearrange("p e j -> p (e j)"))
        for i in range(4, 14, 2):
            weigh(i, 2)
            quantize_w(i - 2, 2)
        for n in range(3):
            group_values(n)
        weigh(14, 1, nc.gpsimd)
        for n in range(3):
            finish(n, nc.sync)
        quantize_w(12, 2)
        for i in (12, 10, 13, 11):
            values(i)
        weigh(15, 1)
        quantize_w(14, 1)
        values(14)
        gated(5, 0, 1)
        quantize_w(15, 1)
        values(15)
        finish(3, nc.sync)
        finish(4, nc.scalar)
        gated(5, 1, 2)
        store(5, nc.sync)
